import numpy as np
CORES = [144,200,272,328,400,456]
N = 6
R, L = 2048, 512
CAPP = 256
def entries(a): return a.T.reshape(-1)
def pack(v, P): return np.ascontiguousarray(np.asarray(v, np.int32).reshape(-1, P).T)
def lists(rng, how):
    n = N * L
    P = rng.permutation(np.repeat(np.arange(N * N), CAPP))[:n]
    if how == "full":
        a, b = rng.permutation(N)[:2]; o = rng.permutation(N * N); o = o[(o // N != a) & (o % N != b)]
        C = np.concatenate([N * a + rng.permutation(np.delete(np.arange(N), b)), [N * a + b], N * rng.permutation(np.delete(np.arange(N), a)) + b, o])[:n // CAPP]
        P = np.repeat(C, CAPP).reshape(N, L)[rng.permutation(N)].reshape(-1)
    h, g = P // N, P % N
    d = np.zeros(n, np.int64)
    for q in range(N): m = np.nonzero(g == q)[0]; d[m] = R * q + np.concatenate([[0, R - 1], 1 + rng.permutation(R - 2)])[:len(m)]
    s = R * h + rng.integers(0, R, n)
    if how == "fork": s = R * h + rng.integers(0, R, N)[h]
    if how == "chain":
        for q in range(N):
            m = np.nonzero(h == q)[0]; w = d[g == q]
            if len(w): s[m] = w[rng.integers(0, len(w), len(m))]
    if how == "gaps":
        z = rng.permutation(N)[:3]; k = (rng.random(n) < 0.5) | (np.arange(n) // L == z[0]) | (h == z[1]) | (g == z[2]); s[k] = -1; d[k] = -1
    return {"src": np.stack([pack(v, 16) for v in s.reshape(N, L)]), "dst": np.stack([pack(v, 16) for v in d.reshape(N, L)])}
def setup_inputs(rng):
    return dict({"tab": rng.standard_normal((N, 128, R), dtype=np.float32)}, **lists(rng, "uniform"))
def setup_inputs_chain(rng):
    d = setup_inputs(rng); d.update(lists(rng, "chain"))
    for k in ("tab",): d[k] = (d[k].astype(np.float32) * 1048576.0).astype(d[k].dtype)
    return d
def setup_inputs_fork(rng):
    d = setup_inputs(rng); d.update(lists(rng, "fork"))
    for k in ("tab",): d[k] = (d[k].astype(np.float32) * (1 / 1024.0)).astype(d[k].dtype)
    return d
def setup_inputs_full(rng):
    d = setup_inputs(rng); d.update(lists(rng, "full"))
    return d
def setup_inputs_gaps(rng):
    d = setup_inputs(rng); d.update(lists(rng, "gaps"))
    return d
def check_inputs(x):
    bad = []; s, d = x["src"].reshape(-1), x["dst"].reshape(-1); k = d >= 0
    if s.min() < -1 or s.max() >= N * R or d.min() < -1 or d.max() >= N * R: bad.append("out of range")
    if ((s < 0) != (d < 0)).any(): bad.append("half a pair")
    if len(np.unique(d[k])) != int(k.sum()): bad.append("a column is written twice")
    if k.any() and int(np.bincount(s[k] // R * N + d[k] // R).max()) > CAPP: bad.append("more than CAPP pairs from one rank's part to one rank's part")
    return bad
def reference(tab, src, dst):
    A = np.concatenate(list(tab), axis=1); Y = A.copy()
    for r in range(N):
        s, d = entries(src[r]), entries(dst[r]); k = d >= 0
        Y[:, d[k]] = A[:, s[k]]
    return {"y": np.stack([Y[:, R * r:R * r + R] for r in range(N)])}

@@ -1,0 +1,454 @@
+from concourse.bass import DstId, RemoteDMATransfer
+from concourse.mybir import AluOpType as Op, ActivationFunctionType as Fn
+
+N, COLS, CAPP = 6, 2048, 256
+CH = 24
+CW = CAPP // 16
+NR = N - 1
+WIN = COLS + 16 + NR * CAPP
+LAND = COLS + 16
+WORLD = 512
+HALF = COLS // 2
+SC0 = 10
+YB = 512
+
+SCRATCH = {
+    "LS": ("dram", [N, 128, 4], "int32"),
+    "LD": ("dram", [N, 128, 4], "int32"),
+    "SD": ("sbuf", [128, 2 * CH], "int32"),
+    "W": ("sbuf", [128, WIN], "float32"),
+    "snd": ("sbuf", [128, 3 * CAPP], "float32"),
+    "yb": ("sbuf", [128, COLS], "float32"),
+    "nio": ("sbuf", [128, 136], "bfloat16"),
+    "m16": ("sbuf", [128, 128], "bfloat16"),
+    "neg": ("sbuf", [128, 128], "bfloat16"),
+    "tri": ("sbuf", [128, 128], "bfloat16"),
+    "ones": ("sbuf", [128, 128], "bfloat16"),
+    "rst": ("sbuf", [128, NR * CH], "bfloat16"),
+    "bia": ("sbuf", [128, NR * CH], "bfloat16"),
+    "tA": ("sbuf", [128, CH], "int32"),
+    "tB": ("sbuf", [128, CH], "int32"),
+    "tF": ("sbuf", [128, CH], "int32"),
+    "sl": ("sbuf", [128, CH], "int32"),
+    "slf": ("sbuf", [128, CH], "float32"),
+    "M": ("sbuf", [128, 3 * CH], "bfloat16"),
+    "I": ("sbuf", [128, 3 * CH], "bfloat16"),
+    "t1": ("sbuf", [128, 3 * CH], "float32"),
+    "xi": ("sbuf", [128, CH], "int32"),
+    "qm": ("sbuf", [128, 2 * CH], "int32"),
+    "qmf": ("sbuf", [128, 2 * CH], "float32"),
+    "L": ("sbuf", [128, CH * 128], "float16"),
+    "R": ("sbuf", [128, CH * 3 * CW], "float16"),
+    "ab": ("sbuf", [128, CH * 3 * CW], "float32"),
+    "off": ("sbuf", [128, 3 * CW], "uint16"),
+    "pm": ("sbuf", [128, 2], "int32"),
+    "pmi": ("sbuf", [128, 2], "int32"),
+    "pmf": ("sbuf", [128, 2], "float32"),
+    "c2a": ("sbuf", [128, 128], "float32"),
+    "c2": ("sbuf", [128, 128], "float32"),
+    "M2": ("sbuf", [128, NR * CH], "bfloat16"),
+    "ML": ("sbuf", [128, CH], "bfloat16"),
+    "I2": ("sbuf", [128, NR * CH], "bfloat16"),
+    "slm": ("sbuf", [128, CH], "float32"),
+    "t2": ("sbuf", [128, N * CH], "float32"),
+    "s1": ("sbuf", [128, 3 * CH], "float32"),
+    "s2": ("sbuf", [128, CH], "float32"),
+    "u": ("sbuf", [128, CH], "float32"),
+    "dq": ("sbuf", [128, 2 * CH], "int32"),
+    "dqf": ("sbuf", [128, 2 * CH], "float32"),
+    "L2": ("sbuf", [128, CH * 128], "float16"),
+    "R2": ("sbuf", [128, CH * 128], "float16"),
+    "e1": ("sbuf", [128, 128], "float32"),
+    "e2": ("sbuf", [128, 128], "float32"),
+    "e3": ("sbuf", [128, 128], "float32"),
+    "inv": ("sbuf", [128, 128], "uint16"),
+    "pA": ("psum", [128, 512], "float32"),
+    "pB": ("psum", [128, 512], "float32"),
+    "pC": ("psum", [128, 512], "float32"),
+    "pD": ("psum", [128, 512], "float32"),
+}
+SEMAPHORES = (["ls", "go", "lb", "tb0", "tb1", "ta", "da", "sent", "ys"] + ["l%d" % a for a in range(N)]
+              + ["c%d" % k for k in range(90)])
+
+_plans = {}
+
+
+def make_plan(cores, topo):
+    key = tuple(cores)
+    if key in _plans:
+        return _plans[key]
+
+    def same(x, z):
+        return topo.host(x) == topo.host(z) and topo.chip(x) == topo.chip(z)
+
+    def rk(x):
+        return topo.rack(topo.host(x))
+
+    used = set(cores)
+    job = {}
+    helpers = {}
+    todo = []
+    for a in range(N):
+        ca = cores[a]
+        direct = [b for b in range(N) if b != a and topo.may_write(ca, cores[b])]
+        rest = [b for b in range(N) if b != a and b not in direct]
+        mine = [c for c in range(WORLD) if c != ca and same(c, ca)]
+        near = [b for b in rest if any(topo.may_write(c, cores[b]) for c in mine)]
+        far = [b for b in rest if b not in near]
+        order = lambda b, ca=ca: (rk(ca) == rk(cores[b]), topo.chip(ca) == topo.chip(cores[b]), b)
+        near.sort(key=order)
+        direct.sort(key=order)
+        job[ca] = (a, direct)
+        able = [c for c in mine if all(topo.may_write(c, cores[b]) for b in near)]
+        other = [c for c in able if topo.die(c) != topo.die(ca)]
+        own = [c for c in able if topo.die(c) == topo.die(ca)]
+        helpers[a] = [other[0]]
+        used.add(other[0])
+        if far:
+            job[other[0]] = (a, near)
+            todo.append((a, far))
+        else:
+            part = [b for b in near if topo.host(cores[b]) == topo.host(ca)]
+            job[other[0]] = (a, [b for b in near if b not in part])
+            job[own[0]] = (a, part)
+            helpers[a].append(own[0])
+            used.add(own[0])
+    for a, far in todo:
+        ca = cores[a]
+        zs = [c for c in range(WORLD) if c not in used and topo.same_plane(c, ca) and topo.chip(c) == topo.chip(ca)
+              and topo.die(c) == topo.die(ca) and all(topo.may_write(c, cores[b]) for b in far)]
+        far.sort(key=lambda b: (topo.chip(cores[b]) == topo.chip(ca), b))
+        job[zs[0]] = (a, far)
+        helpers[a].append(zs[0])
+        used.add(zs[0])
+    need = sorted(job)
+    hop1, relay, calls = {}, {c: [] for c in need}, {c: 0 for c in need}
+    tasks = []
+    for a in range(N):
+        ca = cores[a]
+        hop1[a] = [d for d in need if d != ca and topo.may_write(ca, d)]
+        rest = [d for d in need if d != ca and d not in hop1[a]]
+        chips = {}
+        for d in rest:
+            chips.setdefault((topo.host(d), topo.chip(d)), []).append(d)
+        for ds in chips.values():
+            cand = [w for w in hop1[a] if w not in cores and all(topo.may_write(w, d) for d in ds)]
+            tasks.append((len(cand), a, ds, cand))
+    tasks.sort(key=lambda t: (t[0], t[1]))
+    given = {}
+    for _, a, ds, cand in tasks:
+        def cost(w):
+            new = (w, a) not in given
+            far = rk(w) != rk(ds[0])
+            return (max(calls[w] + new, 2), far, len(given.get((w, a), [])) + len(ds) > 5, calls[w] + new, w)
+        w = min(cand, key=cost)
+        if (w, a) not in given:
+            given[(w, a)] = []
+            calls[w] += 1
+        given[(w, a)] += ds
+    for (w, a), ds in given.items():
+        relay[w].append((a, ds))
+    for w in relay:
+        relay[w].sort(key=lambda e: (not same(cores[e[0]], w), rk(cores[e[0]]) != rk(w), e[0]))
+    p = {"job": job, "helpers": helpers, "hop1": hop1, "relay": relay, "need": need}
+    _plans[key] = p
+    return p
+
+
+def engines(mask):
+    return [e for e in range(16) if (mask >> e) & 1]
+
+
+def bits(es):
+    m = 0
+    for e in es:
+        m |= 1 << e
+    return m
+
+
+def rank_program(g, core, T, topo):
+    plan = make_plan(T.cores, topo)
+    if core not in plan["job"]:
+        return
+    rank = T.rank_of(core)
+    is_rank = rank is not None
+    a, dsts = plan["job"][core]
+    cores = T.cores
+    V, S, PE, Y = g.vector, g.scalar, g.tensor, g.sync
+    sem = T.sem
+    n_sent = [0]
+    stages = []
+
+    def stage():
+        st = {"s": sem["c%d" % len(stages)], "n": 0, "w": False}
+        stages.append(st)
+        return st
+
+    def put(st, ins):
+        ins.then_inc(st["s"], 1)
+        st["n"] += 1
+
+    def need(q, *sts):
+        for st in sts:
+            q.wait_ge(st["s"], st["n"])
+            st["w"] = True
+
+    if is_rank:
+        Y.dma_start(T.LS[a], T.src[:]).then_inc(sem.ls, 16)
+        S.dma_start(T.LD[a], T.dst[:]).then_inc(sem.ls, 16)
+        Y.dma_start(T.W[:, 0:HALF], T.tab[:, 0:HALF]).then_inc(sem.tb0, 16)
+
+    kv, kg, kt = stage(), stage(), stage()
+    put(kv, V.memset(T.neg[:], -1.0))
+    put(kv, V.memset(T.ones[:], 1.0))
+    for i in range(NR):
+        put(kv, V.memset(T.rst[:, CH * i:CH * i + 1], 0.0))
+        put(kv, V.memset(T.rst[:, CH * i + 1:CH * (i + 1)], 1.0))
+        put(kv, V.memset(T.bia[:, CH * i:CH * (i + 1)], (CAPP * i + 16) / 128.0))
+    if is_rank:
+        put(kv, V.memset(T.W[:, COLS:LAND], 0.0))
+    put(kg, g.iota(T.nio[:], [[1, 136]], 0, 0, allow_small_or_imprecise_dtypes=True))
+    put(kg, g.iota(T.m16[:], [[0, 8], [1, 16]], 0, 0, allow_small_or_imprecise_dtypes=True))
+    if is_rank:
+        put(kg, g.iota(T.pm[:], [[0, 2]], 0, 1))
+    need(g, kv)
+    put(kt, g.affine_select(T.tri[:], T.neg[:], [[-1, 128]], Op.is_ge, 0.0, 0, 1))
+
+    def send_lists(r, ds):
+        es = [e for e in engines(topo.mask(core, ds[0])) if all((topo.mask(core, d) >> e) & 1 for d in ds)]
+        ids = []
+        for d in ds:
+            rid, pid = topo.addr(d, core)
+            ids.append(DstId(rid=rid, pnc=pid))
+        tr = []
+        for buf, e in ((T.LS, es[0]), (T.LD, es[2])):
+            tr.append(RemoteDMATransfer(srcs=[buf[r]], dsts=[buf[r]] * len(ds), dst_ids=ids,
+                                        dma_engine_mask=bits([e]), remote_sem=sem["l%d" % r]))
+        g.remote_dma_fused(tr, local_sem=sem.sent)
+        n_sent[0] += 2
+
+    if is_rank:
+        g.wait_ge(sem.ls, 32)
+        send_lists(a, plan["hop1"][a])
+        g.sem_inc(sem.go, 1)
+        Y.wait_ge(sem.go, 1)
+        Y.dma_start(T.W[:, HALF:COLS], T.tab[:, HALF:COLS]).then_inc(sem.tb1, 16)
+    for r, ds in plan["relay"][core]:
+        g.wait_ge(sem["l%d" % r], 2)
+        send_lists(r, ds)
+
+    if is_rank:
+        hs = sorted(plan["helpers"][a], key=lambda h: len(engines(topo.mask(core, h))))
+        taken, masks = [], []
+        for h in hs:
+            es = [e for e in engines(topo.mask(core, h)) if e not in taken][:8]
+            taken += es
+            masks.append(bits(es))
+        for k in range(2):
+            g.wait_ge(sem["tb%d" % k], 16)
+            blk = T.W[:, HALF * k:HALF * (k + 1)]
+            tr = []
+            for h, m in zip(hs, masks):
+                rid, pid = topo.addr(h, core)
+                tr.append(RemoteDMATransfer(srcs=[blk], dsts=[blk], dst_ids=[DstId(rid=rid, pnc=pid)],
+                                            dma_engine_mask=m, remote_sem=sem.ta))
+            g.remote_dma_fused(tr, local_sem=sem.sent)
+            n_sent[0] += 16
+
+    for q, buf, c0 in ((Y, T.LS, 0), (S, T.LD, CH)):
+        if is_rank:
+            q.wait_ge(sem.ls, 32)
+        for r in range(N):
+            if not (is_rank and r == a):
+                q.wait_ge(sem["l%d" % r], 2)
+        q.dma_start(T.SD[:, c0:c0 + CH], buf[:]).then_inc(sem.lb, 16)
+
+    nc = len(dsts)
+    nw = CW * nc
+    src, dst = T.SD[:, 0:CH], T.SD[:, CH:2 * CH]
+    need(PE, kv, kt)
+    ppos = T.pA[:, 0:CH * nc]
+    ps = stage()
+    put(ps, PE.matmul(ppos, T.ones[:], T.bia[:, 0:CH * nc], True, False))
+    if is_rank:
+        ppos2 = T.pC[:, 0:CH * NR]
+        ps2 = stage()
+        put(ps2, PE.matmul(ppos2, T.ones[:], T.bia[:], True, False))
+        k1, k2 = stage(), stage()
+        need(V, kg)
+        put(k1, V.tensor_scalar(T.pmi[:], T.pm[:], 15, None, Op.bitwise_and))
+        put(k1, V.tensor_scalar(T.c2a[:], T.nio[:, 0:128], 16.0, float(COLS), Op.mult, Op.subtract))
+        need(V, k1)
+        put(k2, V.tensor_copy(T.pmf[:], T.pmi[:]))
+        need(V, k2)
+        k3 = stage()
+        put(k3, V.tensor_scalar(T.c2[:], T.c2a[:], T.pmf[:, 0:1], None, Op.add))
+
+    V.wait_ge(sem.lb, 32)
+    d1, d2, d3, d4 = stage(), stage(), stage(), stage()
+    put(d1, V.tensor_scalar(T.tA[:], src, 8, 56, Op.arith_shift_right, Op.bitwise_and))
+    put(d1, V.tensor_scalar(T.tB[:], dst, 11, None, Op.arith_shift_right))
+    need(V, d1)
+    put(d2, V.tensor_tensor(T.tF[:], T.tA[:], T.tB[:], Op.add))
+    put(d4, V.tensor_scalar(T.sl[:], src, COLS - 1, None, Op.bitwise_and))
+    need(V, d2)
+    for i, b in enumerate(dsts):
+        put(d3, V.tensor_scalar(T.M[:, CH * i:CH * (i + 1)], T.tF[:], float(8 * a + b), None, Op.is_equal))
+    need(V, d3, kv)
+    sc = stage()
+    put(sc, V.tensor_tensor_scan(T.I[:, 0:CH * nc], T.rst[:, 0:CH * nc], T.M[:, 0:CH * nc], 0.0, Op.mult, Op.add))
+    need(PE, d3)
+    put(ps, PE.matmul(ppos, T.tri[:], T.M[:, 0:CH * nc], False, False))
+    need(PE, sc)
+    put(ps, PE.matmul(ppos, T.ones[:], T.I[:, 0:CH * nc], False, True))
+    d5 = stage()
+    need(V, d4)
+    put(d5, V.tensor_copy(T.slf[:], T.sl[:]))
+    if is_rank:
+        r1 = stage()
+        put(r1, V.tensor_scalar(T.dq[:, 0:CH], dst, COLS - 1, 4, Op.bitwise_and, Op.arith_shift_right))
+        put(r1, V.tensor_scalar(T.dq[:, CH:2 * CH], dst, 15, None, Op.bitwise_and))
+    need(V, ps)
+    x1, x2, x3, x4 = stage(), stage(), stage(), stage()
+    if nc == 1:
+        put(x2, V.tensor_tensor(T.xi[:], ppos, T.M[:, 0:CH], Op.mult))
+    else:
+        put(x1, V.tensor_tensor(T.t1[:, 0:CH * nc], ppos, T.M[:, 0:CH * nc], Op.mult))
+        need(V, x1)
+        put(x2, V.tensor_tensor(T.xi[:], T.t1[:, 0:CH], T.t1[:, CH:2 * CH], Op.add))
+    need(V, x2)
+    put(x3, V.tensor_scalar(T.qm[:, 0:CH], T.xi[:], 4, None, Op.arith_shift_right))
+    put(x3, V.tensor_scalar(T.qm[:, CH:2 * CH], T.xi[:], 15, None, Op.bitwise_and))
+    need(V, x3)
+    put(x4, V.tensor_copy(T.qmf[:], T.qm[:]))
+    need(V, x4, d5, kg)
+    need(S, x4, kg)
+    sbat = []
+    c0 = SC0
+    for w in (7, 7):
+        b1, b2 = stage(), stage()
+        for c in range(c0, c0 + w):
+            put(b1, S.activation(T.ab[:, c * nw:(c + 1) * nw], T.nio[:, 1:1 + nw], Fn.Abs, bias=T.qmf[:, c:c + 1], scale=-1.0))
+        need(S, b1)
+        put(b2, S.activation(T.R[:, c0 * nw:(c0 + w) * nw], T.ab[:, c0 * nw:(c0 + w) * nw], Fn.Relu, bias=1.0, scale=-1.0))
+        sbat.append(b2)
+        c0 += w
+    vg = []
+
+    def lhs(st, c):
+        put(st, V.tensor_scalar(T.L[:, 128 * c:128 * (c + 1)], T.m16[:], T.qmf[:, CH + c:CH + c + 1], T.slf[:, c:c + 1],
+                                Op.is_equal, Op.mult))
+
+    for lo, hi in ((0, 5), (5, 10), (10, 17), (17, 21), (21, 24)):
+        st = stage()
+        for c in range(lo, hi):
+            lhs(st, c)
+            if c < SC0:
+                put(st, V.tensor_scalar(T.R[:, c * nw:(c + 1) * nw], T.nio[:, 1:1 + nw], T.qmf[:, c:c + 1], None, Op.is_equal))
+        vg.append((st, lo, hi))
+    po = stage()
+    poff = T.pB[:, 0:nw]
+    for st, lo, hi in vg:
+        need(PE, st)
+        if lo == 10:
+            need(PE, sbat[0])
+        if lo == 17:
+            need(PE, sbat[1])
+        for c in range(lo, hi):
+            put(po, PE.matmul(poff, T.L[:, 128 * c:128 * (c + 1)], T.R[:, c * nw:(c + 1) * nw], c == 0, c == CH - 1))
+    if is_rank:
+        r2 = stage()
+        need(V, r1)
+        put(r2, V.tensor_copy(T.dqf[:], T.dq[:]))
+    of = stage()
+    need(V, po)
+    put(of, V.tensor_copy(T.off[:, 0:nw], poff))
+    if is_rank:
+        V.wait_ge(sem.tb0, 16)
+        V.wait_ge(sem.tb1, 16)
+    else:
+        V.wait_ge(sem.ta, 16)
+    need(V, of)
+    for i, b in enumerate(dsts):
+        ga = stage()
+        put(ga, V.tensor_copy(T.snd[:, CAPP * i:CAPP * (i + 1)], T.W[:, 0:COLS].indirect(T.off[:, CW * i:CW * (i + 1)])))
+        d = cores[b]
+        rid, pid = topo.addr(d, core)
+        base = LAND + CAPP * (a if a < b else a - 1)
+        need(g, ga)
+        g.remote_dma(out_ap=T.W[:, base:base + CAPP], in_ap=T.snd[:, CAPP * i:CAPP * (i + 1)], remote_sem=sem.da,
+                     local_sem=sem.sent, pid=pid, routing_id=rid, dma_engine_mask=bits(engines(topo.mask(core, d))[:8]))
+        n_sent[0] += 8
+
+    if is_rank:
+        m1, m2, m3 = stage(), stage(), stage()
+        others = [r for r in range(N) if r != a]
+        for i, r in enumerate(others):
+            put(m1, V.tensor_scalar(T.M2[:, CH * i:CH * (i + 1)], T.tF[:], float(8 * r + a), None, Op.is_equal))
+        put(m3, V.tensor_scalar(T.ML[:], T.tF[:], float(9 * a), None, Op.is_equal))
+        put(m3, V.tensor_scalar(T.slm[:], T.sl[:], float(COLS), None, Op.subtract))
+        need(V, m1)
+        put(m2, V.tensor_tensor_scan(T.I2[:], T.rst[:], T.M2[:], 0.0, Op.mult, Op.add))
+        need(PE, m1)
+        put(ps2, PE.matmul(ppos2, T.tri[:], T.M2[:], False, False))
+        need(PE, m2)
+        put(ps2, PE.matmul(ppos2, T.ones[:], T.I2[:], False, True))
+        need(V, m3, r2)
+        l2 = stage()
+        for c in range(CH):
+            put(l2, V.tensor_scalar(T.L2[:, 128 * c:128 * (c + 1)], T.m16[:], T.dqf[:, CH + c:CH + c + 1], None, Op.is_equal))
+        u1, u2, u3, u4 = stage(), stage(), stage(), stage()
+        put(u1, V.tensor_tensor(T.t2[:, CH * NR:CH * N], T.ML[:], T.slm[:], Op.mult))
+        need(V, ps2)
+        put(u1, V.tensor_tensor(T.t2[:, 0:CH * NR], ppos2, T.M2[:], Op.mult))
+        need(V, u1)
+        put(u2, V.tensor_tensor(T.s1[:], T.t2[:, 0:3 * CH], T.t2[:, 3 * CH:6 * CH], Op.add))
+        need(V, u2)
+        put(u3, V.tensor_tensor(T.s2[:], T.s1[:, 0:CH], T.s1[:, CH:2 * CH], Op.add))
+        need(V, u3)
+        put(u4, V.tensor_tensor(T.u[:], T.s2[:], T.s1[:, 2 * CH:3 * CH], Op.add))
+        need(V, u4)
+        pd = stage()
+        for lo in range(0, CH, 6):
+            st = stage()
+            for c in range(lo, lo + 6):
+                put(st, V.tensor_scalar(T.R2[:, 128 * c:128 * (c + 1)], T.nio[:, 0:128], T.dqf[:, c:c + 1], T.u[:, c:c + 1],
+                                        Op.is_equal, Op.mult))
+            need(PE, st)
+            if lo == 0:
+                need(PE, l2)
+            for c in range(lo, lo + 6):
+                put(pd, PE.matmul(T.pD[:, 0:128], T.L2[:, 128 * c:128 * (c + 1)], T.R2[:, 128 * c:128 * (c + 1)],
+                                  c == 0, c == CH - 1))
+        need(V, pd, k3)
+        f1, f2, f3, f4 = stage(), stage(), stage(), stage()
+        put(f1, V.tensor_scalar(T.e1[:], T.pD[:, 0:128], 0.0, None, Op.is_equal))
+        need(V, f1)
+        put(f2, V.tensor_tensor(T.e2[:], T.e1[:], T.c2[:], Op.mult))
+        need(V, f2)
+        put(f3, V.tensor_tensor(T.e3[:], T.pD[:, 0:128], T.e2[:], Op.add))
+        need(V, f3)
+        put(f4, V.tensor_scalar(T.inv[:], T.e3[:], float(COLS), None, Op.add))
+        need(V, f4)
+        need(S, f4)
+        V.wait_ge(sem.da, 8 * NR)
+        S.wait_ge(sem.da, 8 * NR)
+        S.wait_ge(sem.tb0, 16)
+        S.wait_ge(sem.tb1, 16)
+        ys = 0
+        for k in range(COLS // YB):
+            yk = stage()
+            out = T.yb[:, YB * k:YB * (k + 1)]
+            win = T.W[:].indirect(T.inv[:, YB // 16 * k:YB // 16 * (k + 1)])
+            if k % 2 == 0:
+                put(yk, V.tensor_copy(out, win))
+            else:
+                put(yk, S.activation(out, win, Fn.Copy))
+            need(Y, yk)
+            Y.dma_start(T.y[:, YB * k:YB * (k + 1)], out).then_inc(sem.ys, 16)
+            ys += 16
+        Y.wait_ge(sem.ys, ys)
+    g.wait_ge(sem.sent, n_sent[0])
+    for st in stages:
+        if st["n"] and not st["w"]:
+            need(g, st)

@@ -5,19 +5,23 @@ N, COLS, CAPP = 6, 2048, 256
 CH = 24
 CW = CAPP // 16
 NR = N - 1
-WIN = COLS + 16 + NR * CAPP
 LAND = COLS + 16
+WIN = LAND + NR * CAPP
 WORLD = 512
 HALF = COLS // 2
-SC0 = 10
-YB = 512
+MC = 3
+LE = 2
+YB = (256, 512, 640, 640)
+SB = ((7, 16), (16, 24))
+VB = ((0, 4), (4, 7), (7, 16), (16, 21), (21, 24))
+IB = ((12, 18), (18, 24))
 
 SCRATCH = {
     "LS": ("dram", [N, 128, 4], "int32"),
     "LD": ("dram", [N, 128, 4], "int32"),
     "SD": ("sbuf", [128, 2 * CH], "int32"),
     "W": ("sbuf", [128, WIN], "float32"),
-    "snd": ("sbuf", [128, 3 * CAPP], "float32"),
+    "snd": ("sbuf", [128, 2 * CAPP], "float32"),
     "yb": ("sbuf", [128, COLS], "float32"),
     "nio": ("sbuf", [128, 136], "bfloat16"),
     "m16": ("sbuf", [128, 128], "bfloat16"),
@@ -31,44 +35,40 @@ SCRATCH = {
     "tF": ("sbuf", [128, CH], "int32"),
     "sl": ("sbuf", [128, CH], "int32"),
     "slf": ("sbuf", [128, CH], "float32"),
-    "M": ("sbuf", [128, 3 * CH], "bfloat16"),
-    "I": ("sbuf", [128, 3 * CH], "bfloat16"),
-    "t1": ("sbuf", [128, 3 * CH], "float32"),
+    "M": ("sbuf", [128, NR * CH], "bfloat16"),
+    "I": ("sbuf", [128, NR * CH], "bfloat16"),
+    "t1": ("sbuf", [128, MC * CH], "float32"),
     "xi": ("sbuf", [128, CH], "int32"),
     "qm": ("sbuf", [128, 2 * CH], "int32"),
     "qmf": ("sbuf", [128, 2 * CH], "float32"),
     "L": ("sbuf", [128, CH * 128], "float16"),
-    "R": ("sbuf", [128, CH * 3 * CW], "float16"),
-    "ab": ("sbuf", [128, CH * 3 * CW], "float32"),
-    "off": ("sbuf", [128, 3 * CW], "uint16"),
+    "R": ("sbuf", [128, CH * MC * CW], "float16"),
+    "ab": ("sbuf", [128, CH * MC * CW], "float32"),
+    "off": ("sbuf", [128, MC * CW], "uint16"),
     "pm": ("sbuf", [128, 2], "int32"),
     "pmi": ("sbuf", [128, 2], "int32"),
     "pmf": ("sbuf", [128, 2], "float32"),
     "c2a": ("sbuf", [128, 128], "float32"),
     "c2": ("sbuf", [128, 128], "float32"),
-    "M2": ("sbuf", [128, NR * CH], "bfloat16"),
     "ML": ("sbuf", [128, CH], "bfloat16"),
-    "I2": ("sbuf", [128, NR * CH], "bfloat16"),
     "slm": ("sbuf", [128, CH], "float32"),
     "t2": ("sbuf", [128, N * CH], "float32"),
     "s1": ("sbuf", [128, 3 * CH], "float32"),
     "s2": ("sbuf", [128, CH], "float32"),
     "u": ("sbuf", [128, CH], "float32"),
-    "dq": ("sbuf", [128, 2 * CH], "int32"),
-    "dqf": ("sbuf", [128, 2 * CH], "float32"),
     "L2": ("sbuf", [128, CH * 128], "float16"),
     "R2": ("sbuf", [128, CH * 128], "float16"),
     "e1": ("sbuf", [128, 128], "float32"),
     "e2": ("sbuf", [128, 128], "float32"),
     "e3": ("sbuf", [128, 128], "float32"),
+    "invo": ("sbuf", [128, 128], "uint16"),
     "inv": ("sbuf", [128, 128], "uint16"),
     "pA": ("psum", [128, 512], "float32"),
     "pB": ("psum", [128, 512], "float32"),
-    "pC": ("psum", [128, 512], "float32"),
     "pD": ("psum", [128, 512], "float32"),
 }
-SEMAPHORES = (["ls", "go", "lb", "tb0", "tb1", "ta", "da", "sent", "ys"] + ["l%d" % a for a in range(N)]
-              + ["c%d" % k for k in range(90)])
+SEMAPHORES = (["ls", "iv", "lb", "of", "tb0", "tb1", "ta", "da", "sent", "ys"] + ["l%d" % a for a in range(N)]
+              + ["c%d" % k for k in range(60)])
 
 _plans = {}
 
@@ -78,8 +78,11 @@ def make_plan(cores, topo):
     if key in _plans:
         return _plans[key]
 
+    def place(x):
+        return (topo.host(x), topo.chip(x))
+
     def same(x, z):
-        return topo.host(x) == topo.host(z) and topo.chip(x) == topo.chip(z)
+        return place(x) == place(z)
 
     def rk(x):
         return topo.rack(topo.host(x))
@@ -90,67 +93,84 @@ def make_plan(cores, topo):
     todo = []
     for a in range(N):
         ca = cores[a]
-        direct = [b for b in range(N) if b != a and topo.may_write(ca, cores[b])]
-        rest = [b for b in range(N) if b != a and b not in direct]
+
+        def order(b, ca=ca):
+            return (rk(ca) == rk(cores[b]), topo.chip(ca) == topo.chip(cores[b]), b)
+        direct = sorted([b for b in range(N) if b != a and topo.may_write(ca, cores[b])], key=order)
         mine = [c for c in range(WORLD) if c != ca and same(c, ca)]
-        near = [b for b in rest if any(topo.may_write(c, cores[b]) for c in mine)]
+        rest = [b for b in range(N) if b != a and b not in direct]
+        near = sorted([b for b in rest if any(topo.may_write(c, cores[b]) for c in mine)], key=order)
         far = [b for b in rest if b not in near]
-        order = lambda b, ca=ca: (rk(ca) == rk(cores[b]), topo.chip(ca) == topo.chip(cores[b]), b)
-        near.sort(key=order)
-        direct.sort(key=order)
-        job[ca] = (a, direct)
         able = [c for c in mine if all(topo.may_write(c, cores[b]) for b in near)]
-        other = [c for c in able if topo.die(c) != topo.die(ca)]
-        own = [c for c in able if topo.die(c) == topo.die(ca)]
-        helpers[a] = [other[0]]
-        used.add(other[0])
+        other = [c for c in able if topo.die(c) != topo.die(ca)][0]
+        own = [c for c in able if topo.die(c) == topo.die(ca)][0]
+        job[ca] = (a, direct)
+        helpers[a] = [other]
+        used.add(other)
         if far:
-            job[other[0]] = (a, near)
+            job[other] = (a, near)
             todo.append((a, far))
         else:
-            part = [b for b in near if topo.host(cores[b]) == topo.host(ca)]
-            job[other[0]] = (a, [b for b in near if b not in part])
-            job[own[0]] = (a, part)
-            helpers[a].append(own[0])
-            used.add(own[0])
+            part = [b for b in near if rk(cores[b]) != rk(ca)]
+            job[other] = (a, [b for b in near if b not in part])
+            job[own] = (a, part + direct[:1])
+            job[ca] = (a, direct[1:])
+            helpers[a].append(own)
+            used.add(own)
     for a, far in todo:
         ca = cores[a]
         zs = [c for c in range(WORLD) if c not in used and topo.same_plane(c, ca) and topo.chip(c) == topo.chip(ca)
-              and topo.die(c) == topo.die(ca) and all(topo.may_write(c, cores[b]) for b in far)]
+              and topo.die(c) != topo.die(ca) and all(topo.may_write(c, cores[b]) for b in far)]
         far.sort(key=lambda b: (topo.chip(cores[b]) == topo.chip(ca), b))
         job[zs[0]] = (a, far)
         helpers[a].append(zs[0])
         used.add(zs[0])
-    need = sorted(job)
-    hop1, relay, calls = {}, {c: [] for c in need}, {c: 0 for c in need}
-    tasks = []
+    ship_in = [place(h) for a in range(N) for h in helpers[a] if not same(h, cores[a])]
+    ship_out = [place(cores[a]) for a in range(N) if not all(same(h, cores[a]) for h in helpers[a])]
+    index = {}
     for a in range(N):
         ca = cores[a]
-        hop1[a] = [d for d in need if d != ca and topo.may_write(ca, d)]
-        rest = [d for d in need if d != ca and d not in hop1[a]]
+        vs = [c for c in range(WORLD) if c not in used and same(c, ca) and all(topo.may_write(c, cores[b]) for b in job[helpers[a][0]][1])]
+        vs.sort(key=lambda c: (topo.die(c) == topo.die(ca), c))
+        index[a] = vs[0]
+        job[vs[0]] = (a, [])
+        used.add(vs[0])
+    server = {a: [h for h in helpers[a] if same(h, cores[a])][-1] for a in range(N)}
+    need = sorted(c for c in job if c not in cores)
+    hop1, tasks = {}, []
+    for a in range(N):
+        ca = cores[a]
+        hop1[a] = [d for d in need if topo.may_write(ca, d)]
         chips = {}
-        for d in rest:
-            chips.setdefault((topo.host(d), topo.chip(d)), []).append(d)
+        for d in need:
+            if d not in hop1[a]:
+                chips.setdefault(place(d), []).append(d)
         for ds in chips.values():
-            cand = [w for w in hop1[a] if w not in cores and all(topo.may_write(w, d) for d in ds)]
+            cand = [w for w in hop1[a] if all(topo.may_write(w, d) for d in ds)]
             tasks.append((len(cand), a, ds, cand))
     tasks.sort(key=lambda t: (t[0], t[1]))
-    given = {}
+    given, calls = {}, {c: 0 for c in need}
     for _, a, ds, cand in tasks:
         def cost(w):
             new = (w, a) not in given
+            first = new and calls[w] == 0
             far = rk(w) != rk(ds[0])
-            return (max(calls[w] + new, 2), far, len(given.get((w, a), [])) + len(ds) > 5, calls[w] + new, w)
+            clash = topo.die(w) == topo.die(cores[0]) and not same(w, ds[0]) and (place(ds[0]) in ship_in or place(w) in ship_out)
+            return (clash, not (first and len(job[w][1]) > 0), not first, max(calls[w] + new, 1), far,
+                    len(given.get((w, a), [])) + len(ds) > 5, calls[w] + new, w)
         w = min(cand, key=cost)
         if (w, a) not in given:
             given[(w, a)] = []
             calls[w] += 1
         given[(w, a)] += ds
+    relay = {c: [] for c in job}
     for (w, a), ds in given.items():
         relay[w].append((a, ds))
     for w in relay:
         relay[w].sort(key=lambda e: (not same(cores[e[0]], w), rk(cores[e[0]]) != rk(w), e[0]))
-    p = {"job": job, "helpers": helpers, "hop1": hop1, "relay": relay, "need": need}
+    for a in range(N):
+        hop1[a].sort(key=lambda d, a=a: ((d, a) not in given, d))
+    p = {"job": job, "helpers": helpers, "hop1": hop1, "relay": relay, "index": index, "server": server}
     _plans[key] = p
     return p
 
@@ -170,10 +190,11 @@ def rank_program(g, core, T, topo):
     plan = make_plan(T.cores, topo)
     if core not in plan["job"]:
         return
-    rank = T.rank_of(core)
-    is_rank = rank is not None
+    is_rank = T.rank_of(core) is not None
     a, dsts = plan["job"][core]
     cores = T.cores
+    lent = plan["job"][cores[a]][1] if plan["server"][a] == core else []
+    is_inv = plan["index"][a] == core
     V, S, PE, Y = g.vector, g.scalar, g.tensor, g.sync
     sem = T.sem
     n_sent = [0]
@@ -193,26 +214,24 @@ def rank_program(g, core, T, topo):
             q.wait_ge(st["s"], st["n"])
             st["w"] = True
 
-    if is_rank:
-        Y.dma_start(T.LS[a], T.src[:]).then_inc(sem.ls, 16)
-        S.dma_start(T.LD[a], T.dst[:]).then_inc(sem.ls, 16)
-        Y.dma_start(T.W[:, 0:HALF], T.tab[:, 0:HALF]).then_inc(sem.tb0, 16)
+    def finish():
+        g.wait_ge(sem.sent, n_sent[0])
+        need(g, *[st for st in stages if st["n"] and not st["w"]])
 
-    kv, kg, kt = stage(), stage(), stage()
-    put(kv, V.memset(T.neg[:], -1.0))
-    put(kv, V.memset(T.ones[:], 1.0))
-    for i in range(NR):
-        put(kv, V.memset(T.rst[:, CH * i:CH * i + 1], 0.0))
-        put(kv, V.memset(T.rst[:, CH * i + 1:CH * (i + 1)], 1.0))
-        put(kv, V.memset(T.bia[:, CH * i:CH * (i + 1)], (CAPP * i + 16) / 128.0))
-    if is_rank:
-        put(kv, V.memset(T.W[:, COLS:LAND], 0.0))
-    put(kg, g.iota(T.nio[:], [[1, 136]], 0, 0, allow_small_or_imprecise_dtypes=True))
-    put(kg, g.iota(T.m16[:], [[0, 8], [1, 16]], 0, 0, allow_small_or_imprecise_dtypes=True))
-    if is_rank:
-        put(kg, g.iota(T.pm[:], [[0, 2]], 0, 1))
-    need(g, kv)
-    put(kt, g.affine_select(T.tri[:], T.neg[:], [[-1, 128]], Op.is_ge, 0.0, 0, 1))
+    def send(d, out, in_, rsem, ne):
+        rid, pid = topo.addr(d, core)
+        g.remote_dma(out_ap=out, in_ap=in_, remote_sem=rsem, local_sem=sem.sent, pid=pid, routing_id=rid,
+                     dma_engine_mask=bits(engines(topo.mask(core, d))[:ne]))
+        n_sent[0] += ne
+
+    def send_columns(targets, o):
+        for i, b in enumerate(targets):
+            ga = stage()
+            blk = T.snd[:, CAPP * i:CAPP * (i + 1)]
+            put(ga, V.tensor_copy(blk, T.W[:, 0:COLS].indirect(T.off[:, o + CW * i:o + CW * (i + 1)])))
+            base = LAND + CAPP * (a if a < b else a - 1)
+            need(g, ga)
+            send(cores[b], T.W[:, base:base + CAPP], blk, sem.da, 8)
 
     def send_lists(r, ds):
         es = [e for e in engines(topo.mask(core, ds[0])) if all((topo.mask(core, d) >> e) & 1 for d in ds)]
@@ -221,23 +240,21 @@ def rank_program(g, core, T, topo):
             rid, pid = topo.addr(d, core)
             ids.append(DstId(rid=rid, pnc=pid))
         tr = []
-        for buf, e in ((T.LS, es[0]), (T.LD, es[2])):
+        for buf, e in ((T.LS, es[:LE]), (T.LD, es[LE:2 * LE])):
             tr.append(RemoteDMATransfer(srcs=[buf[r]], dsts=[buf[r]] * len(ds), dst_ids=ids,
-                                        dma_engine_mask=bits([e]), remote_sem=sem["l%d" % r]))
+                                        dma_engine_mask=bits(e), remote_sem=sem["l%d" % r]))
         g.remote_dma_fused(tr, local_sem=sem.sent)
-        n_sent[0] += 2
+        n_sent[0] += 2 * LE
 
+    kv = stage()
     if is_rank:
+        Y.dma_start(T.LS[a], T.src[:]).then_inc(sem.ls, 16)
+        S.dma_start(T.LD[a], T.dst[:]).then_inc(sem.ls, 16)
+        for k in range(2):
+            Y.dma_start(T.W[:, HALF * k:HALF * (k + 1)], T.tab[:, HALF * k:HALF * (k + 1)]).then_inc(sem["tb%d" % k], 16)
+        put(kv, V.memset(T.W[:, COLS:LAND], 0.0))
         g.wait_ge(sem.ls, 32)
         send_lists(a, plan["hop1"][a])
-        g.sem_inc(sem.go, 1)
-        Y.wait_ge(sem.go, 1)
-        Y.dma_start(T.W[:, HALF:COLS], T.tab[:, HALF:COLS]).then_inc(sem.tb1, 16)
-    for r, ds in plan["relay"][core]:
-        g.wait_ge(sem["l%d" % r], 2)
-        send_lists(r, ds)
-
-    if is_rank:
         hs = sorted(plan["helpers"][a], key=lambda h: len(engines(topo.mask(core, h))))
         taken, masks = [], []
         for h in hs:
@@ -254,46 +271,88 @@ def rank_program(g, core, T, topo):
                                             dma_engine_mask=m, remote_sem=sem.ta))
             g.remote_dma_fused(tr, local_sem=sem.sent)
             n_sent[0] += 16
+        for q in (V, S):
+            q.wait_ge(sem.tb0, 16)
+            q.wait_ge(sem.tb1, 16)
+        V.wait_ge(sem.of, 8)
+        send_columns(dsts, 0)
+        need(S, kv)
+        need(V, kv)
+        for q in (V, S):
+            q.wait_ge(sem.iv, 8)
+            q.wait_ge(sem.da, 8 * NR)
+        y0 = 0
+        for k, w in enumerate(YB):
+            yk = stage()
+            out = T.yb[:, y0:y0 + w]
+            win = T.W[:].indirect(T.inv[:, y0 // 16:(y0 + w) // 16])
+            if k % 2 == 0:
+                put(yk, V.tensor_copy(out, win))
+            else:
+                put(yk, S.activation(out, win, Fn.Copy))
+            need(Y, yk)
+            Y.dma_start(T.y[:, y0:y0 + w], out).then_inc(sem.ys, 16)
+            y0 += w
+        Y.wait_ge(sem.ys, 16 * len(YB))
+        finish()
+        return
 
+    kg, kt = stage(), stage()
+    put(kv, V.memset(T.neg[:], -1.0))
+    put(kv, V.memset(T.ones[:], 1.0))
+    for i in range(NR):
+        put(kv, V.memset(T.rst[:, CH * i:CH * i + 1], 0.0))
+        put(kv, V.memset(T.rst[:, CH * i + 1:CH * (i + 1)], 1.0))
+        put(kv, V.memset(T.bia[:, CH * i:CH * (i + 1)], (CAPP * i + 16) / 128.0))
+    put(kg, g.iota(T.nio[:], [[1, 136]], 0, 0, allow_small_or_imprecise_dtypes=True))
+    put(kg, g.iota(T.m16[:], [[0, 8], [1, 16]], 0, 0, allow_small_or_imprecise_dtypes=True))
+    if is_inv:
+        put(kg, g.iota(T.pm[:], [[0, 2]], 0, 1))
+    need(g, kv)
+    put(kt, g.affine_select(T.tri[:], T.neg[:], [[-1, 128]], Op.is_ge, 0.0, 0, 1))
+
+    for r, ds in plan["relay"][core]:
+        g.wait_ge(sem["l%d" % r], 2 * LE)
+        send_lists(r, ds)
     for q, buf, c0 in ((Y, T.LS, 0), (S, T.LD, CH)):
-        if is_rank:
-            q.wait_ge(sem.ls, 32)
         for r in range(N):
-            if not (is_rank and r == a):
-                q.wait_ge(sem["l%d" % r], 2)
+            q.wait_ge(sem["l%d" % r], 2 * LE)
         q.dma_start(T.SD[:, c0:c0 + CH], buf[:]).then_inc(sem.lb, 16)
 
-    nc = len(dsts)
-    nw = CW * nc
     src, dst = T.SD[:, 0:CH], T.SD[:, CH:2 * CH]
+    if is_inv:
+        classes = [8 * r + a for r in range(N) if r != a]
+    else:
+        classes = [8 * a + b for b in lent + dsts]
+    nc = len(classes)
+    nw = CW * nc
     need(PE, kv, kt)
     ppos = T.pA[:, 0:CH * nc]
     ps = stage()
     put(ps, PE.matmul(ppos, T.ones[:], T.bia[:, 0:CH * nc], True, False))
-    if is_rank:
-        ppos2 = T.pC[:, 0:CH * NR]
-        ps2 = stage()
-        put(ps2, PE.matmul(ppos2, T.ones[:], T.bia[:], True, False))
-        k1, k2 = stage(), stage()
+    if is_inv:
+        k1, k2, k3 = stage(), stage(), stage()
         need(V, kg)
         put(k1, V.tensor_scalar(T.pmi[:], T.pm[:], 15, None, Op.bitwise_and))
         put(k1, V.tensor_scalar(T.c2a[:], T.nio[:, 0:128], 16.0, float(COLS), Op.mult, Op.subtract))
         need(V, k1)
         put(k2, V.tensor_copy(T.pmf[:], T.pmi[:]))
         need(V, k2)
-        k3 = stage()
         put(k3, V.tensor_scalar(T.c2[:], T.c2a[:], T.pmf[:, 0:1], None, Op.add))
 
     V.wait_ge(sem.lb, 32)
-    d1, d2, d3, d4 = stage(), stage(), stage(), stage()
+    d1, d2, d3, d4, d5 = stage(), stage(), stage(), stage(), stage()
     put(d1, V.tensor_scalar(T.tA[:], src, 8, 56, Op.arith_shift_right, Op.bitwise_and))
     put(d1, V.tensor_scalar(T.tB[:], dst, 11, None, Op.arith_shift_right))
+    if is_inv:
+        put(d4, V.tensor_scalar(T.qm[:, 0:CH], dst, COLS - 1, 4, Op.bitwise_and, Op.arith_shift_right))
+        put(d4, V.tensor_scalar(T.qm[:, CH:2 * CH], dst, 15, None, Op.bitwise_and))
     need(V, d1)
     put(d2, V.tensor_tensor(T.tF[:], T.tA[:], T.tB[:], Op.add))
     put(d4, V.tensor_scalar(T.sl[:], src, COLS - 1, None, Op.bitwise_and))
     need(V, d2)
-    for i, b in enumerate(dsts):
-        put(d3, V.tensor_scalar(T.M[:, CH * i:CH * (i + 1)], T.tF[:], float(8 * a + b), None, Op.is_equal))
+    for i, k in enumerate(classes):
+        put(d3, V.tensor_scalar(T.M[:, CH * i:CH * (i + 1)], T.tF[:], float(k), None, Op.is_equal))
     need(V, d3, kv)
     sc = stage()
     put(sc, V.tensor_tensor_scan(T.I[:, 0:CH * nc], T.rst[:, 0:CH * nc], T.M[:, 0:CH * nc], 0.0, Op.mult, Op.add))
@@ -301,154 +360,124 @@ def rank_program(g, core, T, topo):
     put(ps, PE.matmul(ppos, T.tri[:], T.M[:, 0:CH * nc], False, False))
     need(PE, sc)
     put(ps, PE.matmul(ppos, T.ones[:], T.I[:, 0:CH * nc], False, True))
-    d5 = stage()
-    need(V, d4)
-    put(d5, V.tensor_copy(T.slf[:], T.sl[:]))
-    if is_rank:
-        r1 = stage()
-        put(r1, V.tensor_scalar(T.dq[:, 0:CH], dst, COLS - 1, 4, Op.bitwise_and, Op.arith_shift_right))
-        put(r1, V.tensor_scalar(T.dq[:, CH:2 * CH], dst, 15, None, Op.bitwise_and))
-    need(V, ps)
-    x1, x2, x3, x4 = stage(), stage(), stage(), stage()
-    if nc == 1:
-        put(x2, V.tensor_tensor(T.xi[:], ppos, T.M[:, 0:CH], Op.mult))
-    else:
-        put(x1, V.tensor_tensor(T.t1[:, 0:CH * nc], ppos, T.M[:, 0:CH * nc], Op.mult))
-        need(V, x1)
-        put(x2, V.tensor_tensor(T.xi[:], T.t1[:, 0:CH], T.t1[:, CH:2 * CH], Op.add))
-    need(V, x2)
-    put(x3, V.tensor_scalar(T.qm[:, 0:CH], T.xi[:], 4, None, Op.arith_shift_right))
-    put(x3, V.tensor_scalar(T.qm[:, CH:2 * CH], T.xi[:], 15, None, Op.bitwise_and))
-    need(V, x3)
-    put(x4, V.tensor_copy(T.qmf[:], T.qm[:]))
-    need(V, x4, d5, kg)
-    need(S, x4, kg)
-    sbat = []
-    c0 = SC0
-    for w in (7, 7):
-        b1, b2 = stage(), stage()
-        for c in range(c0, c0 + w):
-            put(b1, S.activation(T.ab[:, c * nw:(c + 1) * nw], T.nio[:, 1:1 + nw], Fn.Abs, bias=T.qmf[:, c:c + 1], scale=-1.0))
-        need(S, b1)
-        put(b2, S.activation(T.R[:, c0 * nw:(c0 + w) * nw], T.ab[:, c0 * nw:(c0 + w) * nw], Fn.Relu, bias=1.0, scale=-1.0))
-        sbat.append(b2)
-        c0 += w
-    vg = []
+    need(V, d4, kg)
 
-    def lhs(st, c):
-        put(st, V.tensor_scalar(T.L[:, 128 * c:128 * (c + 1)], T.m16[:], T.qmf[:, CH + c:CH + c + 1], T.slf[:, c:c + 1],
-                                Op.is_equal, Op.mult))
-
-    for lo, hi in ((0, 5), (5, 10), (10, 17), (17, 21), (21, 24)):
-        st = stage()
-        for c in range(lo, hi):
-            lhs(st, c)
-            if c < SC0:
-                put(st, V.tensor_scalar(T.R[:, c * nw:(c + 1) * nw], T.nio[:, 1:1 + nw], T.qmf[:, c:c + 1], None, Op.is_equal))
-        vg.append((st, lo, hi))
-    po = stage()
-    poff = T.pB[:, 0:nw]
-    for st, lo, hi in vg:
-        need(PE, st)
-        if lo == 10:
-            need(PE, sbat[0])
-        if lo == 17:
-            need(PE, sbat[1])
-        for c in range(lo, hi):
-            put(po, PE.matmul(poff, T.L[:, 128 * c:128 * (c + 1)], T.R[:, c * nw:(c + 1) * nw], c == 0, c == CH - 1))
-    if is_rank:
-        r2 = stage()
-        need(V, r1)
-        put(r2, V.tensor_copy(T.dqf[:], T.dq[:]))
-    of = stage()
-    need(V, po)
-    put(of, V.tensor_copy(T.off[:, 0:nw], poff))
-    if is_rank:
-        V.wait_ge(sem.tb0, 16)
-        V.wait_ge(sem.tb1, 16)
-    else:
-        V.wait_ge(sem.ta, 16)
-    need(V, of)
-    for i, b in enumerate(dsts):
-        ga = stage()
-        put(ga, V.tensor_copy(T.snd[:, CAPP * i:CAPP * (i + 1)], T.W[:, 0:COLS].indirect(T.off[:, CW * i:CW * (i + 1)])))
-        d = cores[b]
-        rid, pid = topo.addr(d, core)
-        base = LAND + CAPP * (a if a < b else a - 1)
-        need(g, ga)
-        g.remote_dma(out_ap=T.W[:, base:base + CAPP], in_ap=T.snd[:, CAPP * i:CAPP * (i + 1)], remote_sem=sem.da,
-                     local_sem=sem.sent, pid=pid, routing_id=rid, dma_engine_mask=bits(engines(topo.mask(core, d))[:8]))
-        n_sent[0] += 8
-
-    if is_rank:
-        m1, m2, m3 = stage(), stage(), stage()
-        others = [r for r in range(N) if r != a]
-        for i, r in enumerate(others):
-            put(m1, V.tensor_scalar(T.M2[:, CH * i:CH * (i + 1)], T.tF[:], float(8 * r + a), None, Op.is_equal))
-        put(m3, V.tensor_scalar(T.ML[:], T.tF[:], float(9 * a), None, Op.is_equal))
-        put(m3, V.tensor_scalar(T.slm[:], T.sl[:], float(COLS), None, Op.subtract))
-        need(V, m1)
-        put(m2, V.tensor_tensor_scan(T.I2[:], T.rst[:], T.M2[:], 0.0, Op.mult, Op.add))
-        need(PE, m1)
-        put(ps2, PE.matmul(ppos2, T.tri[:], T.M2[:], False, False))
-        need(PE, m2)
-        put(ps2, PE.matmul(ppos2, T.ones[:], T.I2[:], False, True))
-        need(V, m3, r2)
-        l2 = stage()
-        for c in range(CH):
-            put(l2, V.tensor_scalar(T.L2[:, 128 * c:128 * (c + 1)], T.m16[:], T.dqf[:, CH + c:CH + c + 1], None, Op.is_equal))
-        u1, u2, u3, u4 = stage(), stage(), stage(), stage()
-        put(u1, V.tensor_tensor(T.t2[:, CH * NR:CH * N], T.ML[:], T.slm[:], Op.mult))
-        need(V, ps2)
-        put(u1, V.tensor_tensor(T.t2[:, 0:CH * NR], ppos2, T.M2[:], Op.mult))
-        need(V, u1)
-        put(u2, V.tensor_tensor(T.s1[:], T.t2[:, 0:3 * CH], T.t2[:, 3 * CH:6 * CH], Op.add))
-        need(V, u2)
-        put(u3, V.tensor_tensor(T.s2[:], T.s1[:, 0:CH], T.s1[:, CH:2 * CH], Op.add))
-        need(V, u3)
-        put(u4, V.tensor_tensor(T.u[:], T.s2[:], T.s1[:, 2 * CH:3 * CH], Op.add))
-        need(V, u4)
-        pd = stage()
-        for lo in range(0, CH, 6):
+    if not is_inv:
+        put(d5, V.tensor_copy(T.slf[:], T.sl[:]))
+        need(V, ps)
+        x1, x2, x3, x4 = stage(), stage(), stage(), stage()
+        if nc == 1:
+            put(x2, V.tensor_tensor(T.xi[:], ppos, T.M[:, 0:CH], Op.mult))
+        else:
+            put(x1, V.tensor_tensor(T.t1[:, 0:CH * nc], ppos, T.M[:, 0:CH * nc], Op.mult))
+            need(V, x1)
+            if nc == 3:
+                x5 = stage()
+                put(x5, V.tensor_tensor(T.t1[:, 0:CH], T.t1[:, 0:CH], T.t1[:, CH:2 * CH], Op.add))
+                need(V, x5)
+            put(x2, V.tensor_tensor(T.xi[:], T.t1[:, 0:CH], T.t1[:, CH * (nc - 1):CH * nc], Op.add))
+        need(V, x2)
+        put(x3, V.tensor_scalar(T.qm[:, 0:CH], T.xi[:], 4, None, Op.arith_shift_right))
+        put(x3, V.tensor_scalar(T.qm[:, CH:2 * CH], T.xi[:], 15, None, Op.bitwise_and))
+        need(V, x3)
+        put(x4, V.tensor_copy(T.qmf[:], T.qm[:]))
+        need(V, x4, d5)
+        need(S, x4, kg)
+        sbat = {}
+        for lo, hi in SB:
+            b1, b2 = stage(), stage()
+            for c in range(lo, hi):
+                put(b1, S.activation(T.ab[:, c * nw:(c + 1) * nw], T.nio[:, 1:1 + nw], Fn.Abs, bias=T.qmf[:, c:c + 1], scale=-1.0))
+            need(S, b1)
+            put(b2, S.activation(T.R[:, lo * nw:hi * nw], T.ab[:, lo * nw:hi * nw], Fn.Relu, bias=1.0, scale=-1.0))
+            sbat[lo] = b2
+        po = stage()
+        poff = T.pB[:, 0:nw]
+        for lo, hi in VB:
             st = stage()
-            for c in range(lo, lo + 6):
-                put(st, V.tensor_scalar(T.R2[:, 128 * c:128 * (c + 1)], T.nio[:, 0:128], T.dqf[:, c:c + 1], T.u[:, c:c + 1],
+            for c in range(lo, hi):
+                put(st, V.tensor_scalar(T.L[:, 128 * c:128 * (c + 1)], T.m16[:], T.qmf[:, CH + c:CH + c + 1], T.slf[:, c:c + 1],
                                         Op.is_equal, Op.mult))
+                if c < SB[0][0]:
+                    put(st, V.tensor_scalar(T.R[:, c * nw:(c + 1) * nw], T.nio[:, 1:1 + nw], T.qmf[:, c:c + 1], None, Op.is_equal))
             need(PE, st)
-            if lo == 0:
-                need(PE, l2)
-            for c in range(lo, lo + 6):
-                put(pd, PE.matmul(T.pD[:, 0:128], T.L2[:, 128 * c:128 * (c + 1)], T.R2[:, 128 * c:128 * (c + 1)],
-                                  c == 0, c == CH - 1))
-        need(V, pd, k3)
-        f1, f2, f3, f4 = stage(), stage(), stage(), stage()
-        put(f1, V.tensor_scalar(T.e1[:], T.pD[:, 0:128], 0.0, None, Op.is_equal))
-        need(V, f1)
-        put(f2, V.tensor_tensor(T.e2[:], T.e1[:], T.c2[:], Op.mult))
-        need(V, f2)
-        put(f3, V.tensor_tensor(T.e3[:], T.pD[:, 0:128], T.e2[:], Op.add))
-        need(V, f3)
-        put(f4, V.tensor_scalar(T.inv[:], T.e3[:], float(COLS), None, Op.add))
-        need(V, f4)
-        need(S, f4)
-        V.wait_ge(sem.da, 8 * NR)
-        S.wait_ge(sem.da, 8 * NR)
-        S.wait_ge(sem.tb0, 16)
-        S.wait_ge(sem.tb1, 16)
-        ys = 0
-        for k in range(COLS // YB):
-            yk = stage()
-            out = T.yb[:, YB * k:YB * (k + 1)]
-            win = T.W[:].indirect(T.inv[:, YB // 16 * k:YB // 16 * (k + 1)])
-            if k % 2 == 0:
-                put(yk, V.tensor_copy(out, win))
-            else:
-                put(yk, S.activation(out, win, Fn.Copy))
-            need(Y, yk)
-            Y.dma_start(T.y[:, YB * k:YB * (k + 1)], out).then_inc(sem.ys, 16)
-            ys += 16
-        Y.wait_ge(sem.ys, ys)
-    g.wait_ge(sem.sent, n_sent[0])
-    for st in stages:
-        if st["n"] and not st["w"]:
-            need(g, st)
+            if lo in sbat:
+                need(PE, sbat[lo])
+            for c in range(lo, hi):
+                put(po, PE.matmul(poff, T.L[:, 128 * c:128 * (c + 1)], T.R[:, c * nw:(c + 1) * nw], c == 0, c == CH - 1))
+        of = stage()
+        need(V, po)
+        put(of, V.tensor_copy(T.off[:, 0:nw], poff))
+        if lent:
+            need(g, of)
+            w = CW * len(lent)
+            send(cores[a], T.off[:, 0:w], T.off[:, 0:w], sem.of, 8)
+        V.wait_ge(sem.ta, 16)
+        need(V, of)
+        send_columns(dsts, CW * len(lent))
+        finish()
+        return
+
+    x1, m1, m2 = stage(), stage(), stage()
+    put(x1, V.tensor_copy(T.qmf[:], T.qm[:]))
+    put(m1, V.tensor_scalar(T.ML[:], T.tF[:], float(9 * a), None, Op.is_equal))
+    put(m1, V.tensor_scalar(T.slm[:], T.sl[:], float(COLS), None, Op.subtract))
+    need(S, x1, kg)
+    sbat = []
+    for lo, hi in IB:
+        b1, b2 = stage(), stage()
+        for c in range(lo, hi):
+            put(b1, S.activation(T.R2[:, 128 * c:128 * (c + 1)], T.m16[:], Fn.Abs, bias=T.qmf[:, CH + c:CH + c + 1], scale=-1.0))
+        need(S, b1)
+        put(b2, S.activation(T.L2[:, 128 * lo:128 * hi], T.R2[:, 128 * lo:128 * hi], Fn.Relu, bias=1.0, scale=-1.0))
+        sbat.append(b2)
+    need(V, x1, m1)
+    put(m2, V.tensor_tensor(T.t2[:, CH * NR:CH * N], T.ML[:], T.slm[:], Op.mult))
+    l2 = stage()
+
+    def rows(lo, hi):
+        for c in range(lo, hi):
+            put(l2, V.tensor_scalar(T.L2[:, 128 * c:128 * (c + 1)], T.m16[:], T.qmf[:, CH + c:CH + c + 1], None, Op.is_equal))
+
+    rows(0, 4)
+    u1, u2, u3, u4 = stage(), stage(), stage(), stage()
+    need(V, ps, m2)
+    put(u1, V.tensor_tensor(T.t2[:, 0:CH * NR], ppos, T.M[:], Op.mult))
+    rows(4, 6)
+    need(V, u1)
+    put(u2, V.tensor_tensor(T.s1[:], T.t2[:, 0:3 * CH], T.t2[:, 3 * CH:6 * CH], Op.add))
+    rows(6, 8)
+    need(V, u2)
+    put(u3, V.tensor_tensor(T.s2[:], T.s1[:, 0:CH], T.s1[:, CH:2 * CH], Op.add))
+    rows(8, 10)
+    need(V, u3)
+    put(u4, V.tensor_tensor(T.u[:], T.s2[:], T.s1[:, 2 * CH:3 * CH], Op.add))
+    rows(10, IB[0][0])
+    need(V, u4)
+    pd = stage()
+    for j in range(4):
+        st = stage()
+        if j >= 2:
+            need(V, sbat[j - 2])
+        for c in range(6 * j, 6 * j + 6):
+            put(st, V.tensor_scalar(T.R2[:, 128 * c:128 * (c + 1)], T.nio[:, 0:128], T.qmf[:, c:c + 1], T.u[:, c:c + 1],
+                                    Op.is_equal, Op.mult))
+        need(PE, st)
+        if j == 0:
+            need(PE, l2)
+        if j >= 2:
+            need(PE, sbat[j - 2])
+        for c in range(6 * j, 6 * j + 6):
+            put(pd, PE.matmul(T.pD[:, 0:128], T.L2[:, 128 * c:128 * (c + 1)], T.R2[:, 128 * c:128 * (c + 1)], c == 0, c == CH - 1))
+    need(V, pd, k3)
+    f1, f2, f3, f4 = stage(), stage(), stage(), stage()
+    put(f1, V.tensor_scalar(T.e1[:], T.pD[:, 0:128], 0.0, None, Op.is_equal))
+    need(V, f1)
+    put(f2, V.tensor_tensor(T.e2[:], T.e1[:], T.c2[:], Op.mult))
+    need(V, f2)
+    put(f3, V.tensor_tensor(T.e3[:], T.pD[:, 0:128], T.e2[:], Op.add))
+    need(V, f3)
+    put(f4, V.tensor_scalar(T.invo[:], T.e3[:], float(COLS), None, Op.add))
+    need(g, f4)
+    send(cores[a], T.inv[:], T.invo[:], sem.iv, 8)
+    finish()

from concourse.bass import DstId, RemoteDMATransfer
from concourse.mybir import AluOpType as Op, ActivationFunctionType as Fn

N, COLS, CAPP = 6, 2048, 256
CH = 24
CW = CAPP // 16
NR = N - 1
LAND = COLS + 16
WIN = LAND + NR * CAPP
WORLD = 512
HALF = COLS // 2
MC = 3
LE = 2
YB = (256, 512, 640, 640)
SB = ((7, 16), (16, 24))
VB = ((0, 4), (4, 7), (7, 16), (16, 21), (21, 24))
IB = ((12, 18), (18, 24))

SCRATCH = {
    "LS": ("dram", [N, 128, 4], "int32"),
    "LD": ("dram", [N, 128, 4], "int32"),
    "SD": ("sbuf", [128, 2 * CH], "int32"),
    "W": ("sbuf", [128, WIN], "float32"),
    "snd": ("sbuf", [128, 2 * CAPP], "float32"),
    "yb": ("sbuf", [128, COLS], "float32"),
    "nio": ("sbuf", [128, 136], "bfloat16"),
    "m16": ("sbuf", [128, 128], "bfloat16"),
    "neg": ("sbuf", [128, 128], "bfloat16"),
    "tri": ("sbuf", [128, 128], "bfloat16"),
    "ones": ("sbuf", [128, 128], "bfloat16"),
    "rst": ("sbuf", [128, NR * CH], "bfloat16"),
    "bia": ("sbuf", [128, NR * CH], "bfloat16"),
    "tA": ("sbuf", [128, CH], "int32"),
    "tB": ("sbuf", [128, CH], "int32"),
    "tF": ("sbuf", [128, CH], "int32"),
    "sl": ("sbuf", [128, CH], "int32"),
    "slf": ("sbuf", [128, CH], "float32"),
    "M": ("sbuf", [128, NR * CH], "bfloat16"),
    "I": ("sbuf", [128, NR * CH], "bfloat16"),
    "t1": ("sbuf", [128, MC * CH], "float32"),
    "xi": ("sbuf", [128, CH], "int32"),
    "qm": ("sbuf", [128, 2 * CH], "int32"),
    "qmf": ("sbuf", [128, 2 * CH], "float32"),
    "L": ("sbuf", [128, CH * 128], "float16"),
    "R": ("sbuf", [128, CH * MC * CW], "float16"),
    "ab": ("sbuf", [128, CH * MC * CW], "float32"),
    "off": ("sbuf", [128, MC * CW], "uint16"),
    "pm": ("sbuf", [128, 2], "int32"),
    "pmi": ("sbuf", [128, 2], "int32"),
    "pmf": ("sbuf", [128, 2], "float32"),
    "c2a": ("sbuf", [128, 128], "float32"),
    "c2": ("sbuf", [128, 128], "float32"),
    "ML": ("sbuf", [128, CH], "bfloat16"),
    "slm": ("sbuf", [128, CH], "float32"),
    "t2": ("sbuf", [128, N * CH], "float32"),
    "s1": ("sbuf", [128, 3 * CH], "float32"),
    "s2": ("sbuf", [128, CH], "float32"),
    "u": ("sbuf", [128, CH], "float32"),
    "L2": ("sbuf", [128, CH * 128], "float16"),
    "R2": ("sbuf", [128, CH * 128], "float16"),
    "e1": ("sbuf", [128, 128], "float32"),
    "e2": ("sbuf", [128, 128], "float32"),
    "e3": ("sbuf", [128, 128], "float32"),
    "invo": ("sbuf", [128, 128], "uint16"),
    "inv": ("sbuf", [128, 128], "uint16"),
    "pA": ("psum", [128, 512], "float32"),
    "pB": ("psum", [128, 512], "float32"),
    "pD": ("psum", [128, 512], "float32"),
}
SEMAPHORES = (["ls", "iv", "lb", "of", "tb0", "tb1", "ta", "da", "sent", "ys"] + ["l%d" % a for a in range(N)]
              + ["c%d" % k for k in range(60)])

_plans = {}


def make_plan(cores, topo):
    key = tuple(cores)
    if key in _plans:
        return _plans[key]

    def place(x):
        return (topo.host(x), topo.chip(x))

    def same(x, z):
        return place(x) == place(z)

    def rk(x):
        return topo.rack(topo.host(x))

    used = set(cores)
    job = {}
    helpers = {}
    todo = []
    for a in range(N):
        ca = cores[a]

        def order(b, ca=ca):
            return (rk(ca) == rk(cores[b]), topo.chip(ca) == topo.chip(cores[b]), b)
        direct = sorted([b for b in range(N) if b != a and topo.may_write(ca, cores[b])], key=order)
        mine = [c for c in range(WORLD) if c != ca and same(c, ca)]
        rest = [b for b in range(N) if b != a and b not in direct]
        near = sorted([b for b in rest if any(topo.may_write(c, cores[b]) for c in mine)], key=order)
        far = [b for b in rest if b not in near]
        able = [c for c in mine if all(topo.may_write(c, cores[b]) for b in near)]
        other = [c for c in able if topo.die(c) != topo.die(ca)][0]
        own = [c for c in able if topo.die(c) == topo.die(ca)][0]
        job[ca] = (a, direct)
        helpers[a] = [other]
        used.add(other)
        if far:
            job[other] = (a, near)
            todo.append((a, far))
        else:
            part = [b for b in near if rk(cores[b]) != rk(ca)]
            job[other] = (a, [b for b in near if b not in part])
            job[own] = (a, part + direct[:1])
            job[ca] = (a, direct[1:])
            helpers[a].append(own)
            used.add(own)
    for a, far in todo:
        ca = cores[a]
        zs = [c for c in range(WORLD) if c not in used and topo.same_plane(c, ca) and topo.chip(c) == topo.chip(ca)
              and topo.die(c) != topo.die(ca) and all(topo.may_write(c, cores[b]) for b in far)]
        far.sort(key=lambda b: (topo.chip(cores[b]) == topo.chip(ca), b))
        job[zs[0]] = (a, far)
        helpers[a].append(zs[0])
        used.add(zs[0])
    ship_in = [place(h) for a in range(N) for h in helpers[a] if not same(h, cores[a])]
    ship_out = [place(cores[a]) for a in range(N) if not all(same(h, cores[a]) for h in helpers[a])]
    index = {}
    for a in range(N):
        ca = cores[a]
        vs = [c for c in range(WORLD) if c not in used and same(c, ca) and all(topo.may_write(c, cores[b]) for b in job[helpers[a][0]][1])]
        vs.sort(key=lambda c: (topo.die(c) == topo.die(ca), c))
        index[a] = vs[0]
        job[vs[0]] = (a, [])
        used.add(vs[0])
    server = {a: [h for h in helpers[a] if same(h, cores[a])][-1] for a in range(N)}
    need = sorted(c for c in job if c not in cores)
    hop1, tasks = {}, []
    for a in range(N):
        ca = cores[a]
        hop1[a] = [d for d in need if topo.may_write(ca, d)]
        chips = {}
        for d in need:
            if d not in hop1[a]:
                chips.setdefault(place(d), []).append(d)
        for ds in chips.values():
            cand = [w for w in hop1[a] if all(topo.may_write(w, d) for d in ds)]
            tasks.append((len(cand), a, ds, cand))
    tasks.sort(key=lambda t: (t[0], t[1]))
    given, calls = {}, {c: 0 for c in need}
    for _, a, ds, cand in tasks:
        def cost(w):
            new = (w, a) not in given
            first = new and calls[w] == 0
            far = rk(w) != rk(ds[0])
            clash = topo.die(w) == topo.die(cores[0]) and not same(w, ds[0]) and (place(ds[0]) in ship_in or place(w) in ship_out)
            return (clash, not (first and len(job[w][1]) > 0), not first, max(calls[w] + new, 1), far,
                    len(given.get((w, a), [])) + len(ds) > 5, calls[w] + new, w)
        w = min(cand, key=cost)
        if (w, a) not in given:
            given[(w, a)] = []
            calls[w] += 1
        given[(w, a)] += ds
    relay = {c: [] for c in job}
    for (w, a), ds in given.items():
        relay[w].append((a, ds))
    for w in relay:
        relay[w].sort(key=lambda e: (not same(cores[e[0]], w), rk(cores[e[0]]) != rk(w), e[0]))
    for a in range(N):
        hop1[a].sort(key=lambda d, a=a: ((d, a) not in given, d))
    p = {"job": job, "helpers": helpers, "hop1": hop1, "relay": relay, "index": index, "server": server}
    _plans[key] = p
    return p


def engines(mask):
    return [e for e in range(16) if (mask >> e) & 1]


def bits(es):
    m = 0
    for e in es:
        m |= 1 << e
    return m


def rank_program(g, core, T, topo):
    plan = make_plan(T.cores, topo)
    if core not in plan["job"]:
        return
    is_rank = T.rank_of(core) is not None
    a, dsts = plan["job"][core]
    cores = T.cores
    lent = plan["job"][cores[a]][1] if plan["server"][a] == core else []
    is_inv = plan["index"][a] == core
    V, S, PE, Y = g.vector, g.scalar, g.tensor, g.sync
    sem = T.sem
    n_sent = [0]
    stages = []

    def stage():
        st = {"s": sem["c%d" % len(stages)], "n": 0, "w": False}
        stages.append(st)
        return st

    def put(st, ins):
        ins.then_inc(st["s"], 1)
        st["n"] += 1

    def need(q, *sts):
        for st in sts:
            q.wait_ge(st["s"], st["n"])
            st["w"] = True

    def finish():
        g.wait_ge(sem.sent, n_sent[0])
        need(g, *[st for st in stages if st["n"] and not st["w"]])

    def send(d, out, in_, rsem, ne):
        rid, pid = topo.addr(d, core)
        g.remote_dma(out_ap=out, in_ap=in_, remote_sem=rsem, local_sem=sem.sent, pid=pid, routing_id=rid,
                     dma_engine_mask=bits(engines(topo.mask(core, d))[:ne]))
        n_sent[0] += ne

    def send_columns(targets, o):
        for i, b in enumerate(targets):
            ga = stage()
            blk = T.snd[:, CAPP * i:CAPP * (i + 1)]
            put(ga, V.tensor_copy(blk, T.W[:, 0:COLS].indirect(T.off[:, o + CW * i:o + CW * (i + 1)])))
            base = LAND + CAPP * (a if a < b else a - 1)
            need(g, ga)
            send(cores[b], T.W[:, base:base + CAPP], blk, sem.da, 8)

    def send_lists(r, ds):
        es = [e for e in engines(topo.mask(core, ds[0])) if all((topo.mask(core, d) >> e) & 1 for d in ds)]
        ids = []
        for d in ds:
            rid, pid = topo.addr(d, core)
            ids.append(DstId(rid=rid, pnc=pid))
        tr = []
        for buf, e in ((T.LS, es[:LE]), (T.LD, es[LE:2 * LE])):
            tr.append(RemoteDMATransfer(srcs=[buf[r]], dsts=[buf[r]] * len(ds), dst_ids=ids,
                                        dma_engine_mask=bits(e), remote_sem=sem["l%d" % r]))
        g.remote_dma_fused(tr, local_sem=sem.sent)
        n_sent[0] += 2 * LE

    kv = stage()
    if is_rank:
        Y.dma_start(T.LS[a], T.src[:]).then_inc(sem.ls, 16)
        S.dma_start(T.LD[a], T.dst[:]).then_inc(sem.ls, 16)
        for k in range(2):
            Y.dma_start(T.W[:, HALF * k:HALF * (k + 1)], T.tab[:, HALF * k:HALF * (k + 1)]).then_inc(sem["tb%d" % k], 16)
        put(kv, V.memset(T.W[:, COLS:LAND], 0.0))
        g.wait_ge(sem.ls, 32)
        send_lists(a, plan["hop1"][a])
        hs = sorted(plan["helpers"][a], key=lambda h: len(engines(topo.mask(core, h))))
        taken, masks = [], []
        for h in hs:
            es = [e for e in engines(topo.mask(core, h)) if e not in taken][:8]
            taken += es
            masks.append(bits(es))
        for k in range(2):
            g.wait_ge(sem["tb%d" % k], 16)
            blk = T.W[:, HALF * k:HALF * (k + 1)]
            tr = []
            for h, m in zip(hs, masks):
                rid, pid = topo.addr(h, core)
                tr.append(RemoteDMATransfer(srcs=[blk], dsts=[blk], dst_ids=[DstId(rid=rid, pnc=pid)],
                                            dma_engine_mask=m, remote_sem=sem.ta))
            g.remote_dma_fused(tr, local_sem=sem.sent)
            n_sent[0] += 16
        for q in (V, S):
            q.wait_ge(sem.tb0, 16)
            q.wait_ge(sem.tb1, 16)
        V.wait_ge(sem.of, 8)
        send_columns(dsts, 0)
        need(S, kv)
        need(V, kv)
        for q in (V, S):
            q.wait_ge(sem.iv, 8)
            q.wait_ge(sem.da, 8 * NR)
        y0 = 0
        for k, w in enumerate(YB):
            yk = stage()
            out = T.yb[:, y0:y0 + w]
            win = T.W[:].indirect(T.inv[:, y0 // 16:(y0 + w) // 16])
            if k % 2 == 0:
                put(yk, V.tensor_copy(out, win))
            else:
                put(yk, S.activation(out, win, Fn.Copy))
            need(Y, yk)
            Y.dma_start(T.y[:, y0:y0 + w], out).then_inc(sem.ys, 16)
            y0 += w
        Y.wait_ge(sem.ys, 16 * len(YB))
        finish()
        return

    kg, kt = stage(), stage()
    put(kv, V.memset(T.neg[:], -1.0))
    put(kv, V.memset(T.ones[:], 1.0))
    for i in range(NR):
        put(kv, V.memset(T.rst[:, CH * i:CH * i + 1], 0.0))
        put(kv, V.memset(T.rst[:, CH * i + 1:CH * (i + 1)], 1.0))
        put(kv, V.memset(T.bia[:, CH * i:CH * (i + 1)], (CAPP * i + 16) / 128.0))
    put(kg, g.iota(T.nio[:], [[1, 136]], 0, 0, allow_small_or_imprecise_dtypes=True))
    put(kg, g.iota(T.m16[:], [[0, 8], [1, 16]], 0, 0, allow_small_or_imprecise_dtypes=True))
    if is_inv:
        put(kg, g.iota(T.pm[:], [[0, 2]], 0, 1))
    need(g, kv)
    put(kt, g.affine_select(T.tri[:], T.neg[:], [[-1, 128]], Op.is_ge, 0.0, 0, 1))

    for r, ds in plan["relay"][core]:
        g.wait_ge(sem["l%d" % r], 2 * LE)
        send_lists(r, ds)
    for q, buf, c0 in ((Y, T.LS, 0), (S, T.LD, CH)):
        for r in range(N):
            q.wait_ge(sem["l%d" % r], 2 * LE)
        q.dma_start(T.SD[:, c0:c0 + CH], buf[:]).then_inc(sem.lb, 16)

    src, dst = T.SD[:, 0:CH], T.SD[:, CH:2 * CH]
    if is_inv:
        classes = [8 * r + a for r in range(N) if r != a]
    else:
        classes = [8 * a + b for b in lent + dsts]
    nc = len(classes)
    nw = CW * nc
    need(PE, kv, kt)
    ppos = T.pA[:, 0:CH * nc]
    ps = stage()
    put(ps, PE.matmul(ppos, T.ones[:], T.bia[:, 0:CH * nc], True, False))
    if is_inv:
        k1, k2, k3 = stage(), stage(), stage()
        need(V, kg)
        put(k1, V.tensor_scalar(T.pmi[:], T.pm[:], 15, None, Op.bitwise_and))
        put(k1, V.tensor_scalar(T.c2a[:], T.nio[:, 0:128], 16.0, float(COLS), Op.mult, Op.subtract))
        need(V, k1)
        put(k2, V.tensor_copy(T.pmf[:], T.pmi[:]))
        need(V, k2)
        put(k3, V.tensor_scalar(T.c2[:], T.c2a[:], T.pmf[:, 0:1], None, Op.add))

    V.wait_ge(sem.lb, 32)
    d1, d2, d3, d4, d5 = stage(), stage(), stage(), stage(), stage()
    put(d1, V.tensor_scalar(T.tA[:], src, 8, 56, Op.arith_shift_right, Op.bitwise_and))
    put(d1, V.tensor_scalar(T.tB[:], dst, 11, None, Op.arith_shift_right))
    if is_inv:
        put(d4, V.tensor_scalar(T.qm[:, 0:CH], dst, COLS - 1, 4, Op.bitwise_and, Op.arith_shift_right))
        put(d4, V.tensor_scalar(T.qm[:, CH:2 * CH], dst, 15, None, Op.bitwise_and))
    need(V, d1)
    put(d2, V.tensor_tensor(T.tF[:], T.tA[:], T.tB[:], Op.add))
    put(d4, V.tensor_scalar(T.sl[:], src, COLS - 1, None, Op.bitwise_and))
    need(V, d2)
    for i, k in enumerate(classes):
        put(d3, V.tensor_scalar(T.M[:, CH * i:CH * (i + 1)], T.tF[:], float(k), None, Op.is_equal))
    need(V, d3, kv)
    sc = stage()
    put(sc, V.tensor_tensor_scan(T.I[:, 0:CH * nc], T.rst[:, 0:CH * nc], T.M[:, 0:CH * nc], 0.0, Op.mult, Op.add))
    need(PE, d3)
    put(ps, PE.matmul(ppos, T.tri[:], T.M[:, 0:CH * nc], False, False))
    need(PE, sc)
    put(ps, PE.matmul(ppos, T.ones[:], T.I[:, 0:CH * nc], False, True))
    need(V, d4, kg)

    if not is_inv:
        put(d5, V.tensor_copy(T.slf[:], T.sl[:]))
        need(V, ps)
        x1, x2, x3, x4 = stage(), stage(), stage(), stage()
        if nc == 1:
            put(x2, V.tensor_tensor(T.xi[:], ppos, T.M[:, 0:CH], Op.mult))
        else:
            put(x1, V.tensor_tensor(T.t1[:, 0:CH * nc], ppos, T.M[:, 0:CH * nc], Op.mult))
            need(V, x1)
            if nc == 3:
                x5 = stage()
                put(x5, V.tensor_tensor(T.t1[:, 0:CH], T.t1[:, 0:CH], T.t1[:, CH:2 * CH], Op.add))
                need(V, x5)
            put(x2, V.tensor_tensor(T.xi[:], T.t1[:, 0:CH], T.t1[:, CH * (nc - 1):CH * nc], Op.add))
        need(V, x2)
        put(x3, V.tensor_scalar(T.qm[:, 0:CH], T.xi[:], 4, None, Op.arith_shift_right))
        put(x3, V.tensor_scalar(T.qm[:, CH:2 * CH], T.xi[:], 15, None, Op.bitwise_and))
        need(V, x3)
        put(x4, V.tensor_copy(T.qmf[:], T.qm[:]))
        need(V, x4, d5)
        need(S, x4, kg)
        sbat = {}
        for lo, hi in SB:
            b1, b2 = stage(), stage()
            for c in range(lo, hi):
                put(b1, S.activation(T.ab[:, c * nw:(c + 1) * nw], T.nio[:, 1:1 + nw], Fn.Abs, bias=T.qmf[:, c:c + 1], scale=-1.0))
            need(S, b1)
            put(b2, S.activation(T.R[:, lo * nw:hi * nw], T.ab[:, lo * nw:hi * nw], Fn.Relu, bias=1.0, scale=-1.0))
            sbat[lo] = b2
        po = stage()
        poff = T.pB[:, 0:nw]
        for lo, hi in VB:
            st = stage()
            for c in range(lo, hi):
                put(st, V.tensor_scalar(T.L[:, 128 * c:128 * (c + 1)], T.m16[:], T.qmf[:, CH + c:CH + c + 1], T.slf[:, c:c + 1],
                                        Op.is_equal, Op.mult))
                if c < SB[0][0]:
                    put(st, V.tensor_scalar(T.R[:, c * nw:(c + 1) * nw], T.nio[:, 1:1 + nw], T.qmf[:, c:c + 1], None, Op.is_equal))
            need(PE, st)
            if lo in sbat:
                need(PE, sbat[lo])
            for c in range(lo, hi):
                put(po, PE.matmul(poff, T.L[:, 128 * c:128 * (c + 1)], T.R[:, c * nw:(c + 1) * nw], c == 0, c == CH - 1))
        of = stage()
        need(V, po)
        put(of, V.tensor_copy(T.off[:, 0:nw], poff))
        if lent:
            need(g, of)
            w = CW * len(lent)
            send(cores[a], T.off[:, 0:w], T.off[:, 0:w], sem.of, 8)
        V.wait_ge(sem.ta, 16)
        need(V, of)
        send_columns(dsts, CW * len(lent))
        finish()
        return

    x1, m1, m2 = stage(), stage(), stage()
    put(x1, V.tensor_copy(T.qmf[:], T.qm[:]))
    put(m1, V.tensor_scalar(T.ML[:], T.tF[:], float(9 * a), None, Op.is_equal))
    put(m1, V.tensor_scalar(T.slm[:], T.sl[:], float(COLS), None, Op.subtract))
    need(S, x1, kg)
    sbat = []
    for lo, hi in IB:
        b1, b2 = stage(), stage()
        for c in range(lo, hi):
            put(b1, S.activation(T.R2[:, 128 * c:128 * (c + 1)], T.m16[:], Fn.Abs, bias=T.qmf[:, CH + c:CH + c + 1], scale=-1.0))
        need(S, b1)
        put(b2, S.activation(T.L2[:, 128 * lo:128 * hi], T.R2[:, 128 * lo:128 * hi], Fn.Relu, bias=1.0, scale=-1.0))
        sbat.append(b2)
    need(V, x1, m1)
    put(m2, V.tensor_tensor(T.t2[:, CH * NR:CH * N], T.ML[:], T.slm[:], Op.mult))
    l2 = stage()

    def rows(lo, hi):
        for c in range(lo, hi):
            put(l2, V.tensor_scalar(T.L2[:, 128 * c:128 * (c + 1)], T.m16[:], T.qmf[:, CH + c:CH + c + 1], None, Op.is_equal))

    rows(0, 4)
    u1, u2, u3, u4 = stage(), stage(), stage(), stage()
    need(V, ps, m2)
    put(u1, V.tensor_tensor(T.t2[:, 0:CH * NR], ppos, T.M[:], Op.mult))
    rows(4, 6)
    need(V, u1)
    put(u2, V.tensor_tensor(T.s1[:], T.t2[:, 0:3 * CH], T.t2[:, 3 * CH:6 * CH], Op.add))
    rows(6, 8)
    need(V, u2)
    put(u3, V.tensor_tensor(T.s2[:], T.s1[:, 0:CH], T.s1[:, CH:2 * CH], Op.add))
    rows(8, 10)
    need(V, u3)
    put(u4, V.tensor_tensor(T.u[:], T.s2[:], T.s1[:, 2 * CH:3 * CH], Op.add))
    rows(10, IB[0][0])
    need(V, u4)
    pd = stage()
    for j in range(4):
        st = stage()
        if j >= 2:
            need(V, sbat[j - 2])
        for c in range(6 * j, 6 * j + 6):
            put(st, V.tensor_scalar(T.R2[:, 128 * c:128 * (c + 1)], T.nio[:, 0:128], T.qmf[:, c:c + 1], T.u[:, c:c + 1],
                                    Op.is_equal, Op.mult))
        need(PE, st)
        if j == 0:
            need(PE, l2)
        if j >= 2:
            need(PE, sbat[j - 2])
        for c in range(6 * j, 6 * j + 6):
            put(pd, PE.matmul(T.pD[:, 0:128], T.L2[:, 128 * c:128 * (c + 1)], T.R2[:, 128 * c:128 * (c + 1)], c == 0, c == CH - 1))
    need(V, pd, k3)
    f1, f2, f3, f4 = stage(), stage(), stage(), stage()
    put(f1, V.tensor_scalar(T.e1[:], T.pD[:, 0:128], 0.0, None, Op.is_equal))
    need(V, f1)
    put(f2, V.tensor_tensor(T.e2[:], T.e1[:], T.c2[:], Op.mult))
    need(V, f2)
    put(f3, V.tensor_tensor(T.e3[:], T.pD[:, 0:128], T.e2[:], Op.add))
    need(V, f3)
    put(f4, V.tensor_scalar(T.invo[:], T.e3[:], float(COLS), None, Op.add))
    need(g, f4)
    send(cores[a], T.inv[:], T.invo[:], sem.iv, 8)
    finish()
